import numpy as np
import ml_dtypes


def mxq(x, axis, fmt="e4m3"):
    dtype, down = {"e4m3": (ml_dtypes.float8_e4m3fn, 7), "e5m2": (ml_dtypes.float8_e5m2, 14)}[fmt]
    v = np.moveaxis(np.asarray(x, np.float32).astype(ml_dtypes.bfloat16).astype(np.float64), axis, -1)
    blocks = v.reshape(v.shape[:-1] + (-1, 32))
    amax = np.abs(blocks).max(-1, keepdims=True)
    byte = np.maximum(np.where(amax > 0, np.frexp(amax)[1] - 1 + 127, 0) - down, 1)
    scale = np.exp2(byte - 127.0)
    codes = (blocks / scale).astype(np.float32).astype(dtype).astype(np.float64)
    return np.moveaxis((codes * scale).reshape(v.shape), -1, axis)


WIDE = False


def mx_kscale(k):
    if not WIDE:
        return np.ones(k)
    levels = np.array([10, -10, 5, -5, 0])
    if k % 512:
        return np.exp2(np.random.permutation(np.resize(levels, k // 32))).repeat(32)
    a = np.empty((k // 512, 16))
    for p in range(k // 512):
        a[p, :8] = np.random.permutation(np.resize(levels, 8))
        for g in range(8):
            far = levels[np.abs(levels - a[p, g]) >= 10]
            a[p, g + 8] = far[np.random.randint(len(far))]
    return np.exp2(a.ravel()).repeat(32)


def f64(x):
    return np.asarray(x).astype(np.float64)


def striped(idx):
    return np.tile(idx.reshape(-1, 16).T, (8, 1)).astype(np.uint16)


def unstriped(offs):
    return offs[:16].T.reshape(-1).astype(np.int64)


E2M1 = np.array([0.0, 0.5, 1.0, 1.5, 2.0, 3.0, 4.0, 6.0, -0.0, -0.5, -1.0, -1.5, -2.0, -3.0, -4.0, -6.0])


def pack_weight(w, fmt):
    k, n = w.shape
    w = f64(np.asarray(w, np.float32).astype(ml_dtypes.bfloat16)).reshape(k // 32, 32, n)
    amax = np.abs(w).max(1)
    if fmt == "e4m3":
        byte = np.frexp(amax)[1] - 1 + 127 - 7
    else:
        mant, ex = np.frexp(amax / 6.0)
        byte = np.where(mant > 0.5, ex, ex - 1) + 127
    byte = np.clip(np.where(amax > 0, byte, 1), 1, 254)
    scaled = (w * np.exp2(127.0 - byte)[:, None, :]).reshape(k, n).astype(np.float32)
    by_word = np.ascontiguousarray(scaled.reshape(k // 512, 128, 4, n).transpose(0, 1, 3, 2))
    if fmt == "e4m3":
        words = by_word.astype(ml_dtypes.float8_e4m3fn).view(np.uint8)
    else:
        c = by_word.astype(ml_dtypes.float4_e2m1fn).view(np.uint8) & 0xF
        words = (c[..., 0::2] | (c[..., 1::2] << 4)).reshape(k // 512, 128, 2 * n)
    return np.ascontiguousarray(words), np.ascontiguousarray(byte.astype(np.uint8).reshape(k // 512, 16, n))


def unpack_weight(words, scales, fmt):
    g, _, n = scales.shape
    words = np.ascontiguousarray(words).reshape(g, 128, n, -1)
    if fmt == "e4m3":
        vals = words.view(ml_dtypes.float8_e4m3fn).astype(np.float64)
    else:
        nib = np.empty((g, 128, n, 4), np.uint8)
        nib[..., 0::2] = words & 0xF
        nib[..., 1::2] = words >> 4
        vals = E2M1[nib]
    vals = vals * np.repeat(np.exp2(scales.astype(np.float64) - 127.0), 8, axis=1)[..., None]
    return vals.transpose(0, 1, 3, 2).reshape(g * 512, n)


def gelu(v):
    return 0.5 * v * (1.0 + np.tanh(np.sqrt(2.0 / np.pi) * (v + 0.044715 * v**3)))


K, T, S, P, H, N = 1024, 2048, 1024, 512, 1024, 512

def setup_inputs():
    n = np.random.standard_normal
    s = mx_kscale(K)[:, None]
    u = mx_kscale(H)[:, None]
    perm = np.random.permutation(S)
    tab_words, tab_scales = pack_weight(n((K, T)) * s, "e4m3")
    w2_words, w2_scales = pack_weight(1.2 * n((H, N)) / np.sqrt(H) / u, "e2m1")
    return {
        "tab_words": tab_words, "tab_scales": tab_scales,
        "offs": striped(np.random.permutation(T)[:S]),
        "pos1": striped(perm[:P]),
        "pos2": striped(perm[P:]),
        "w1": (n((K, H)) / np.sqrt(K) / s).astype(np.float32),
        "low": (0.4 * n(H) - 0.3).astype(np.float32),
        "steep": np.random.uniform(1, 3, H).astype(np.float32),
        "share": np.random.uniform(0.1, 0.5, H).astype(np.float32),
        "mix": (2.0 * n((H, P))).astype(np.float32),
        "skip": n(H).astype(np.float32),
        "wgs": np.exp(0.3 * n((128, P))).astype(np.float32),
        "gain": (0.9 * np.exp(0.3 * n(H)) * u[:, 0]).astype(np.float32),
        "w2_words": w2_words, "w2_scales": w2_scales,
        "w3": (1.5 * n((H, N)) / np.sqrt(H) / u).astype(np.float32),
        "shift": (0.8 * n((N, S))).astype(np.float32),
    }

def reference(tab_words, tab_scales, offs, pos1, pos2, w1, low, steep, share, mix, skip, wgs, gain, w2_words, w2_scales, w3, shift):
    v = unpack_weight(tab_words, tab_scales, "e4m3")[:, unstriped(offs)]
    x = mxq(f64(w1), 0, "e4m3").T @ v
    h = np.maximum(x, f64(low)[:, None])
    top = h.max(axis=1)
    a = 1.0 / (1.0 + np.exp(-f64(steep)[:, None] * (h[:, unstriped(pos1)] - f64(share)[:, None] * top[:, None])))
    a = a * f64(mix)
    page = f64(skip)[:, None] * h
    page[:, unstriped(pos2)] = np.tile(f64(wgs), (H // 128, 1)) * a
    pq = mxq(page * f64(gain)[:, None], 0, "e4m3")
    y = unpack_weight(w2_words, w2_scales, "e2m1").T @ pq
    d = mxq(f64(w3), 0, "e4m3").T @ pq
    return y + np.tanh(d + f64(shift))

@@ -1,0 +1,324 @@
+from contextlib import ExitStack
+
+import concourse.mybir as mybir
+
+K, T, S, PICK, H, N = 1024, 2048, 1024, 512, 1024, 512
+FLOPS = 2 * K * H * S + 2 * 2 * H * N * S
+
+F32 = mybir.dt.float32
+BF16 = mybir.dt.bfloat16
+I32 = mybir.dt.int32
+U32 = mybir.dt.uint32
+U16 = mybir.dt.uint16
+U8 = mybir.dt.uint8
+FP8X4 = mybir.dt.float8_e4m3fn_x4
+FP4X4 = mybir.dt.float4_e2m1fn_x4
+ALU = mybir.AluOpType
+ACT = mybir.ActivationFunctionType
+
+P = 128
+PACK = 4
+KP = P * PACK
+BANK = 512
+QUADS = (0, 2, 1, 3)
+
+
+def tile_list_tipburn_tray_readout_kernel(
+    tc, tab_words, tab_scales, offs, pos1, pos2, w1, low, steep, share, mix, skip, wgs, gain,
+    w2_words, w2_scales, w3, shift, out,
+):
+    nc = tc.nc
+    with ExitStack() as ctx:
+        keep = ctx.enter_context(tc.tile_pool(name="keep", bufs=1))
+        ring = ctx.enter_context(tc.tile_pool(name="ring", bufs=2))
+        psum = ctx.enter_context(tc.psum_pool(name="psum", bufs=8))
+
+        tab_sc = keep.tile([P, T], U8, name="tab_sc", align_bytes=64)
+        nc.vector.memset(tab_sc[:].bitcast(I32), 0)
+        for q in QUADS:
+            nc.scalar.dma_start(
+                out=tab_sc[32 * q : 32 * q + 8, :].bitcast(I32),
+                in_=tab_scales[:, 4 * q : 4 * q + 4, :].bitcast(I32),
+            )
+        tab_w = [keep.tile([P, T], I32, name="tab_w%d" % a, align_bytes=64) for a in range(2)]
+        offs_t = keep.tile([P, S // 16], U16, name="offs_t")
+        pos1_t = keep.tile([P, PICK // 16], U16, name="pos1_t")
+        pos2_t = keep.tile([P, PICK // 16], U16, name="pos2_t")
+        nc.sync.dma_start(out=tab_w[0][:], in_=tab_words[0].rearrange("p t i -> p (t i)").bitcast(I32))
+        nc.sync.dma_start(offs_t[:], offs)
+        nc.sync.dma_start(out=tab_w[1][:], in_=tab_words[1].rearrange("p t i -> p (t i)").bitcast(I32))
+
+        def load_rows(name, vec):
+            t = keep.tile([P, H // P], F32, name=name)
+            nc.gpsimd.dma_start(
+                out=t[:].rearrange("p (b i) -> p b i", i=PACK),
+                in_=vec.rearrange("(b p i) -> p b i", p=P, i=PACK),
+            )
+            return t
+
+        low_t = load_rows("low_t", low)
+        steep_t = load_rows("steep_t", steep)
+        share_t = load_rows("share_t", share)
+        skip_t = load_rows("skip_t", skip)
+        gain_t = load_rows("gain_t", gain)
+
+        HALF = KP // 2
+
+        def load_w(w, a, c0, name):
+            raw = keep.tile([P, PACK, HALF], F32, name=name, tag="raw", bufs=8)
+            nc.sync.dma_start(
+                out=raw[:],
+                in_=w[KP * a : KP * (a + 1), c0 : c0 + HALF].rearrange("(p j) c -> p j c", j=PACK),
+            )
+            return raw
+
+        w1_raw = {}
+        for a in range(2):
+            for c in range(2):
+                w1_raw[0, a, c] = load_w(w1, a, c * HALF, "w1_raw0%d%d" % (a, c))
+        nc.sync.dma_start(pos1_t[:], pos1)
+        nc.sync.dma_start(pos2_t[:], pos2)
+
+        wgs_t = [keep.tile([P, 2, PICK], F32, name="wgs_t%d" % u) for u in range(2)]
+        mix_t = {}
+
+        def load_wgs(u):
+            rows = wgs.rearrange("(q i) m -> q i m", i=PACK)[:, 2 * u : 2 * u + 2, :]
+            for q in QUADS:
+                nc.sync.dma_start(out=wgs_t[u][32 * q : 32 * q + 32, :, :], in_=rows)
+
+        def load_mix(b, u):
+            mix_t[b, u] = keep.tile([P, 2, PICK], F32, name="mix_t%d%d" % (b, u))
+            rows = mix[KP * b : KP * (b + 1), :].rearrange("(p i) m -> p i m", i=PACK)
+            nc.sync.dma_start(out=mix_t[b, u][:], in_=rows[:, 2 * u : 2 * u + 2, :])
+
+        load_wgs(0)
+        load_mix(0, 0)
+        for a in range(2):
+            for c in range(2):
+                w1_raw[1, a, c] = load_w(w1, a, KP + c * HALF, "w1_raw1%d%d" % (a, c))
+        load_wgs(1)
+        load_mix(0, 1)
+        for u in range(2):
+            load_mix(1, u)
+
+        w3_raw = {}
+        for b in range(2):
+            for c in range(2):
+                w3_raw[b, c] = load_w(w3, b, c * HALF, "w3_raw%d%d" % (b, c))
+        w2_w = keep.tile([P, 2, 2 * N], U8, name="w2_w", align_bytes=64)
+        w2_sc = keep.tile([P, 2, N], U8, name="w2_sc", align_bytes=64)
+        nc.vector.memset(w2_sc[:].rearrange("p a c -> p (a c)").bitcast(I32), 0)
+        nc.sync.dma_start(out=w2_w[:].bitcast(I32), in_=w2_words.rearrange("a p c -> p a c").bitcast(I32))
+        for q in QUADS:
+            nc.sync.dma_start(
+                out=w2_sc[32 * q : 32 * q + 4, :, :].bitcast(I32),
+                in_=w2_scales[:, 4 * q : 4 * q + 4, :].rearrange("a r c -> r a c").bitcast(I32),
+            )
+        shift_t = []
+        for nt in range(N // P):
+            st = keep.tile([P, S], F32, name="shift_t%d" % nt)
+            nc.sync.dma_start(out=st[:], in_=shift[P * nt : P * (nt + 1), :])
+            shift_t.append(st)
+
+        got_w = [keep.tile([P, S], U32, name="got_w%d" % a, align_bytes=64) for a in range(2)]
+        got_sc = keep.tile([P, S], U8, name="got_sc", align_bytes=64)
+        nc.vector.tensor_copy(got_w[0][:], tab_w[0][:].bitcast(U32).indirect(offs_t[:]))
+        nc.vector.tensor_copy(got_sc[:], tab_sc[:].indirect(offs_t[:]))
+        nc.vector.tensor_copy(got_w[1][:], tab_w[1][:].bitcast(U32).indirect(offs_t[:]))
+
+        slope = keep.tile([P, H // P], F32, name="slope")
+        minus = keep.tile([P, H // P], F32, name="minus")
+        nc.gpsimd.tensor_scalar(out=minus[:], in0=steep_t[:], scalar1=-1.0, scalar2=0.0, op0=ALU.mult, op1=ALU.add)
+        nc.gpsimd.tensor_tensor(slope[:], minus[:], share_t[:], ALU.mult)
+
+        w_bf = {}
+        w1_q, w1_sc, w3_q, w3_sc = {}, {}, {}, {}
+
+        def bf_tile(key):
+            if key not in w_bf:
+                w_bf[key] = ring.tile([P, KP * PACK], BF16, name="w_bf", align_bytes=64)
+            return w_bf[key]
+
+        def cast_w1(b, a, c, copy):
+            dst = bf_tile(("w1", b, a))[:].rearrange("p (t m j) -> p m j t", t=PACK, j=PACK)
+            m = HALF // PACK
+            copy(
+                out=dst[:, c * m : (c + 1) * m],
+                in_=w1_raw[b, a, c][:].rearrange("p j (m t) -> p m j t", t=PACK),
+            )
+
+        def quant_w1(b, a, parts):
+            w1_q[b, a] = keep.tile([P, KP], U32, name="w1_q%d%d" % (b, a), align_bytes=64)
+            w1_sc[b, a] = keep.tile([P, KP], U8, name="w1_sc%d%d" % (b, a), align_bytes=64)
+            w = KP // parts
+            for s in range(parts):
+                nc.vector.quantize_mx(
+                    out=w1_q[b, a][:, s * w : (s + 1) * w].bitcast(FP8X4),
+                    scales=w1_sc[b, a][:, s * w : (s + 1) * w],
+                    in_=w_bf["w1", b, a][:, PACK * s * w : PACK * (s + 1) * w],
+                )
+
+        def cast_w3(b, c):
+            dst = bf_tile(("w3", b))[:].rearrange("p (m t j) -> p m j t", t=PACK, j=PACK)
+            m = HALF // PACK
+            nc.scalar.copy(
+                out=dst[:, c * m : (c + 1) * m],
+                in_=w3_raw[b, c][:].rearrange("p j (m t) -> p m j t", t=PACK),
+            )
+
+        def quant_w3(b):
+            w3_q[b] = keep.tile([P, N], U32, name="w3_q%d" % b, align_bytes=64)
+            w3_sc[b] = keep.tile([P, N], U8, name="w3_sc%d" % b, align_bytes=64)
+            nc.vector.quantize_mx(out=w3_q[b][:].bitcast(FP8X4), scales=w3_sc[b][:], in_=w_bf["w3", b][:])
+
+        cast_w1(0, 0, 0, nc.scalar.copy)
+        cast_w1(0, 0, 1, nc.scalar.copy)
+        quant_w1(0, 0, 1)
+        cast_w1(0, 1, 0, nc.scalar.copy)
+        cast_w1(0, 1, 1, nc.vector.tensor_copy)
+        quant_w1(0, 1, PACK)
+
+        tops = keep.tile([P, 2 * (H // P)], F32, name="tops")
+        bias = keep.tile([P, H // P], F32, name="bias")
+        h_t, look_t, page_t, weight_t = {}, {}, {}, {}
+        pairs = {}
+        b_q = [keep.tile([P, S], U32, name="b_q%d" % b, align_bytes=64) for b in range(2)]
+        b_sc = [keep.tile([P, S], U8, name="b_sc%d" % b, align_bytes=64) for b in range(2)]
+
+        def first_product(r):
+            b, i = divmod(r, PACK)
+            h_t[r] = ring.tile([P, S], F32, name="h")
+            for half in range(2):
+                cols = slice(half * BANK, (half + 1) * BANK)
+                acc = psum.tile([P, BANK], F32, name="acc")
+                for a in range(2):
+                    nc.tensor.matmul_mx(
+                        out=acc[:],
+                        lhsT=w1_q[b, a][:, i * P : (i + 1) * P].bitcast(FP8X4),
+                        lhsT_scale=w1_sc[b, a][:, i * P : (i + 1) * P],
+                        rhs=got_w[a][:, cols].bitcast(FP8X4),
+                        rhs_scale=got_sc[PACK * a : P, cols],
+                        start=(a == 0),
+                        stop=(a == 1),
+                    )
+                nc.vector.tensor_scalar(
+                    out=h_t[r][:, cols], in0=acc[:], scalar1=low_t[:, r : r + 1], scalar2=None,
+                    op0=ALU.max, op1=ALU.max, accum_out=tops[:, 2 * r + half : 2 * r + half + 1],
+                )
+            nc.vector.tensor_scalar(
+                out=bias[:, r : r + 1], in0=tops[:, 2 * r : 2 * r + 1],
+                scalar1=tops[:, 2 * r + 1 : 2 * r + 2], scalar2=slope[:, r : r + 1],
+                op0=ALU.max, op1=ALU.mult,
+            )
+
+        def weights_of(r):
+            b, i = divmod(r, PACK)
+            weight_t[r] = ring.tile([P, PICK], F32, name="weight")
+            nc.vector.tensor_tensor(weight_t[r][:], mix_t[b, i // 2][:, i % 2, :], wgs_t[i // 2][:, i % 2, :], ALU.mult)
+
+        def look_and_fill(r):
+            look_t[r] = ring.tile([P, PICK], F32, name="look")
+            nc.scalar.activation(
+                out=look_t[r][:], in_=h_t[r][:].indirect(pos1_t[:]), func=ACT.Sigmoid,
+                bias=bias[:, r : r + 1], scale=steep_t[:, r : r + 1],
+            )
+            page_t[r] = ring.tile([P, S], F32, name="page", bufs=4)
+            nc.scalar.activation(out=page_t[r][:], in_=h_t[r][:], func=ACT.Copy, scale=skip_t[:, r : r + 1])
+
+        def put(r):
+            nc.vector.tensor_tensor(page_t[r][:].indirect(pos2_t[:]), look_t[r][:], weight_t[r][:], ALU.mult)
+
+        def round_page(r):
+            b, i = divmod(r, PACK)
+            for half in range(2):
+                if i == 0:
+                    pairs[b, half] = ring.tile([P, 2, BANK, 2], BF16, name="pairs", bufs=4)
+                nc.scalar.activation(
+                    out=pairs[b, half][:, i // 2, :, i % 2], in_=page_t[r][:, half * BANK : (half + 1) * BANK],
+                    func=ACT.Copy, scale=gain_t[:, r : r + 1],
+                )
+
+        def quant_page(b, half):
+            cols = slice(half * BANK, (half + 1) * BANK)
+            woven = ring.tile([P, BANK * PACK], BF16, name="woven", align_bytes=64)
+            nc.vector.tensor_copy(
+                out=woven[:].bitcast(F32).rearrange("p (c e u) -> p c u e", e=PACK, u=2),
+                in_=pairs[b, half][:].rearrange("p u c k -> p (u c k)").bitcast(F32).rearrange("p (u c e) -> p c u e", u=2, e=PACK),
+            )
+            nc.vector.quantize_mx(out=b_q[b][:, cols].bitcast(FP8X4), scales=b_sc[b][:, cols], in_=woven[:])
+
+        tiles = H // P
+        rounds = ((), (), (0,), (1,), (2, 3), (4,), (5,), (6,))
+        first_product(0)
+        first_product(1)
+        for r in range(tiles):
+            weights_of(r)
+            look_and_fill(r)
+            if r in (1, 2):
+                cast_w1(1, r - 1, 0, nc.scalar.copy)
+                cast_w1(1, r - 1, 1, nc.scalar.copy)
+                quant_w1(1, r - 1, 1)
+            for done in rounds[r]:
+                round_page(done)
+            if r >= 4:
+                cast_w3(*divmod(r - 4, 2))
+            put(r)
+            if r + 2 < tiles:
+                first_product(r + 2)
+            if r in (5, 7):
+                quant_w3(r // 6)
+            if r == 6:
+                quant_page(0, 0)
+        round_page(tiles - 1)
+        quant_page(0, 1)
+
+        acc_y, acc_d, inner, bent = {}, {}, {}, {}
+
+        def second_pass(c, b):
+            half, nt = divmod(c, N // P)
+            cols = slice(half * BANK, (half + 1) * BANK)
+            if b == 0:
+                acc_d[c] = psum.tile([P, BANK], F32, name="acc")
+                acc_y[c] = psum.tile([P, BANK], F32, name="acc")
+            nc.tensor.matmul_mx(
+                out=acc_d[c][:],
+                lhsT=w3_q[b][:, nt * P : (nt + 1) * P].bitcast(FP8X4),
+                lhsT_scale=w3_sc[b][:, nt * P : (nt + 1) * P],
+                rhs=b_q[b][:, cols].bitcast(FP8X4), rhs_scale=b_sc[b][:, cols],
+                start=(b == 0), stop=(b == 1),
+            )
+            nc.tensor.matmul_mx(
+                out=acc_y[c][:],
+                lhsT=w2_w[:, b, 2 * nt * P : 2 * (nt + 1) * P].bitcast(FP4X4),
+                lhsT_scale=w2_sc[:, b, nt * P : (nt + 1) * P],
+                rhs=b_q[b][:, cols].bitcast(FP8X4), rhs_scale=b_sc[b][:, cols],
+                start=(b == 0), stop=(b == 1),
+            )
+
+        def shift_and_bend(c):
+            half, nt = divmod(c, N // P)
+            inner[c] = ring.tile([P, BANK], F32, name="inner")
+            nc.vector.tensor_tensor(inner[c][:], acc_d[c][:], shift_t[nt][:, half * BANK : (half + 1) * BANK], ALU.add)
+            bent[c] = ring.tile([P, BANK], F32, name="bent", bufs=3)
+            nc.scalar.activation(out=bent[c][:], in_=inner[c][:], func=ACT.Tanh)
+
+        def finish(c):
+            half, nt = divmod(c, N // P)
+            res = ring.tile([P, BANK], F32, name="res", bufs=4)
+            nc.vector.tensor_tensor(res[:], acc_y[c][:], bent[c][:], ALU.add)
+            nc.sync.dma_start(out=out[nt * P : (nt + 1) * P, half * BANK : (half + 1) * BANK], in_=res[:])
+
+        chunks = 2 * (N // P)
+        for c in range(N // P):
+            second_pass(c, 0)
+        quant_page(1, 0)
+        quant_page(1, 1)
+        for c in range(chunks):
+            if c >= N // P:
+                second_pass(c, 0)
+            second_pass(c, 1)
+            shift_and_bend(c)
+            if c > 0:
+                finish(c - 1)
+        finish(chunks - 1)

@@ -34,33 +34,28 @@ def tile_list_tipburn_tray_readout_kernel(
         psum = ctx.enter_context(tc.psum_pool(name="psum", bufs=8))
 
         tab_sc = keep.tile([P, T], U8, name="tab_sc", align_bytes=64)
-        nc.vector.memset(tab_sc[:].bitcast(I32), 0)
+        nc.gpsimd.memset(tab_sc[:].bitcast(I32), 0)
+        tab_w = [keep.tile([P, T], I32, name="tab_w%d" % a, align_bytes=64) for a in range(2)]
+        offs_t = keep.tile([P, S // 16], U16, name="offs_t")
+        pos1_t = keep.tile([P, PICK // 16], U16, name="pos1_t")
+        pos2_t = keep.tile([P, PICK // 16], U16, name="pos2_t")
+        nc.sync.dma_start(offs_t[:], offs)
+        nc.sync.dma_start(out=tab_w[0][:], in_=tab_words[0].rearrange("p t i -> p (t i)").bitcast(I32))
         for q in QUADS:
             nc.scalar.dma_start(
                 out=tab_sc[32 * q : 32 * q + 8, :].bitcast(I32),
                 in_=tab_scales[:, 4 * q : 4 * q + 4, :].bitcast(I32),
             )
-        tab_w = [keep.tile([P, T], I32, name="tab_w%d" % a, align_bytes=64) for a in range(2)]
-        offs_t = keep.tile([P, S // 16], U16, name="offs_t")
-        pos1_t = keep.tile([P, PICK // 16], U16, name="pos1_t")
-        pos2_t = keep.tile([P, PICK // 16], U16, name="pos2_t")
-        nc.sync.dma_start(out=tab_w[0][:], in_=tab_words[0].rearrange("p t i -> p (t i)").bitcast(I32))
-        nc.sync.dma_start(offs_t[:], offs)
         nc.sync.dma_start(out=tab_w[1][:], in_=tab_words[1].rearrange("p t i -> p (t i)").bitcast(I32))
 
         def load_rows(name, vec):
             t = keep.tile([P, H // P], F32, name=name)
-            nc.gpsimd.dma_start(
+            nc.sync.dma_start(
                 out=t[:].rearrange("p (b i) -> p b i", i=PACK),
                 in_=vec.rearrange("(b p i) -> p b i", p=P, i=PACK),
             )
             return t
 
-        low_t = load_rows("low_t", low)
-        steep_t = load_rows("steep_t", steep)
-        share_t = load_rows("share_t", share)
-        skip_t = load_rows("skip_t", skip)
-        gain_t = load_rows("gain_t", gain)
 
         HALF = KP // 2
 
@@ -76,7 +71,11 @@ def tile_list_tipburn_tray_readout_kernel(
         for a in range(2):
             for c in range(2):
                 w1_raw[0, a, c] = load_w(w1, a, c * HALF, "w1_raw0%d%d" % (a, c))
+        low_t = load_rows("low_t", low)
+        steep_t = load_rows("steep_t", steep)
+        share_t = load_rows("share_t", share)
         nc.sync.dma_start(pos1_t[:], pos1)
+        skip_t = load_rows("skip_t", skip)
         nc.sync.dma_start(pos2_t[:], pos2)
 
         wgs_t = [keep.tile([P, 2, PICK], F32, name="wgs_t%d" % u) for u in range(2)]
@@ -92,11 +91,13 @@ def tile_list_tipburn_tray_readout_kernel(
             rows = mix[KP * b : KP * (b + 1), :].rearrange("(p i) m -> p i m", i=PACK)
             nc.sync.dma_start(out=mix_t[b, u][:], in_=rows[:, 2 * u : 2 * u + 2, :])
 
+        for c in range(2):
+            w1_raw[1, 0, c] = load_w(w1, 0, KP + c * HALF, "w1_raw10%d" % c)
         load_wgs(0)
         load_mix(0, 0)
-        for a in range(2):
-            for c in range(2):
-                w1_raw[1, a, c] = load_w(w1, a, KP + c * HALF, "w1_raw1%d%d" % (a, c))
+        gain_t = load_rows("gain_t", gain)
+        for c in range(2):
+            w1_raw[1, 1, c] = load_w(w1, 1, KP + c * HALF, "w1_raw11%d" % c)
         load_wgs(1)
         load_mix(0, 1)
         for u in range(2):
@@ -108,7 +109,7 @@ def tile_list_tipburn_tray_readout_kernel(
                 w3_raw[b, c] = load_w(w3, b, c * HALF, "w3_raw%d%d" % (b, c))
         w2_w = keep.tile([P, 2, 2 * N], U8, name="w2_w", align_bytes=64)
         w2_sc = keep.tile([P, 2, N], U8, name="w2_sc", align_bytes=64)
-        nc.vector.memset(w2_sc[:].rearrange("p a c -> p (a c)").bitcast(I32), 0)
+        nc.gpsimd.memset(w2_sc[:].rearrange("p a c -> p (a c)").bitcast(I32), 0)
         nc.sync.dma_start(out=w2_w[:].bitcast(I32), in_=w2_words.rearrange("a p c -> p a c").bitcast(I32))
         for q in QUADS:
             nc.sync.dma_start(
@@ -137,7 +138,7 @@ def tile_list_tipburn_tray_readout_kernel(
 
         def bf_tile(key):
             if key not in w_bf:
-                w_bf[key] = ring.tile([P, KP * PACK], BF16, name="w_bf", align_bytes=64)
+                w_bf[key] = ring.tile([P, KP * PACK], BF16, name="w_bf", align_bytes=64, bufs=3)
             return w_bf[key]
 
         def cast_w1(b, a, c, copy):
@@ -151,12 +152,11 @@ def tile_list_tipburn_tray_readout_kernel(
         def quant_w1(b, a, parts):
             w1_q[b, a] = keep.tile([P, KP], U32, name="w1_q%d%d" % (b, a), align_bytes=64)
             w1_sc[b, a] = keep.tile([P, KP], U8, name="w1_sc%d%d" % (b, a), align_bytes=64)
-            w = KP // parts
-            for s in range(parts):
+            for lo, hi in parts:
                 nc.vector.quantize_mx(
-                    out=w1_q[b, a][:, s * w : (s + 1) * w].bitcast(FP8X4),
-                    scales=w1_sc[b, a][:, s * w : (s + 1) * w],
-                    in_=w_bf["w1", b, a][:, PACK * s * w : PACK * (s + 1) * w],
+                    out=w1_q[b, a][:, lo:hi].bitcast(FP8X4),
+                    scales=w1_sc[b, a][:, lo:hi],
+                    in_=w_bf["w1", b, a][:, PACK * lo : PACK * hi],
                 )
 
         def cast_w3(b, c):
@@ -174,21 +174,20 @@ def tile_list_tipburn_tray_readout_kernel(
 
         cast_w1(0, 0, 0, nc.scalar.copy)
         cast_w1(0, 0, 1, nc.scalar.copy)
-        quant_w1(0, 0, 1)
+        quant_w1(0, 0, [(0, KP)])
         cast_w1(0, 1, 0, nc.scalar.copy)
         cast_w1(0, 1, 1, nc.vector.tensor_copy)
-        quant_w1(0, 1, PACK)
+        quant_w1(0, 1, [(0, P), (P, KP)])
 
         tops = keep.tile([P, 2 * (H // P)], F32, name="tops")
         bias = keep.tile([P, H // P], F32, name="bias")
         h_t, look_t, page_t, weight_t = {}, {}, {}, {}
         pairs = {}
-        b_q = [keep.tile([P, S], U32, name="b_q%d" % b, align_bytes=64) for b in range(2)]
-        b_sc = [keep.tile([P, S], U8, name="b_sc%d" % b, align_bytes=64) for b in range(2)]
+        woven, b_q, b_sc = {}, {}, {}
 
         def first_product(r):
             b, i = divmod(r, PACK)
-            h_t[r] = ring.tile([P, S], F32, name="h")
+            h_t[r] = keep.tile([P, S], F32, name="h", tag="turn%d" % ((r + 1) % 4), align_bytes=64)
             for half in range(2):
                 cols = slice(half * BANK, (half + 1) * BANK)
                 acc = psum.tile([P, BANK], F32, name="acc")
@@ -214,11 +213,12 @@ def tile_list_tipburn_tray_readout_kernel(
 
         def weights_of(r):
             b, i = divmod(r, PACK)
-            weight_t[r] = ring.tile([P, PICK], F32, name="weight")
-            nc.vector.tensor_tensor(weight_t[r][:], mix_t[b, i // 2][:, i % 2, :], wgs_t[i // 2][:, i % 2, :], ALU.mult)
+            weight_t[r] = keep.tile([P, PICK], F32, name="weight", tag="weight%d" % (r % 2), align_bytes=64)
+            engine = nc.vector if r == H // P - 1 else nc.gpsimd
+            engine.tensor_tensor(weight_t[r][:], mix_t[b, i // 2][:, i % 2, :], wgs_t[i // 2][:, i % 2, :], ALU.mult)
 
         def look_and_fill(r):
-            look_t[r] = ring.tile([P, PICK], F32, name="look")
+            look_t[r] = keep.tile([P, PICK], F32, name="look", tag="turn%d" % (r % 4), align_bytes=64)
             nc.scalar.activation(
                 out=look_t[r][:], in_=h_t[r][:].indirect(pos1_t[:]), func=ACT.Sigmoid,
                 bias=bias[:, r : r + 1], scale=steep_t[:, r : r + 1],
@@ -239,66 +239,78 @@ def tile_list_tipburn_tray_readout_kernel(
                     func=ACT.Copy, scale=gain_t[:, r : r + 1],
                 )
 
-        def quant_page(b, half):
-            cols = slice(half * BANK, (half + 1) * BANK)
-            woven = ring.tile([P, BANK * PACK], BF16, name="woven", align_bytes=64)
-            nc.vector.tensor_copy(
-                out=woven[:].bitcast(F32).rearrange("p (c e u) -> p c u e", e=PACK, u=2),
+        def weave_page(b, half, copy, tag):
+            woven[b, half] = keep.tile([P, BANK * PACK], BF16, name="woven", tag=tag, align_bytes=64)
+            copy(
+                out=woven[b, half][:].bitcast(F32).rearrange("p (c e u) -> p c u e", e=PACK, u=2),
                 in_=pairs[b, half][:].rearrange("p u c k -> p (u c k)").bitcast(F32).rearrange("p (u c e) -> p c u e", u=2, e=PACK),
             )
-            nc.vector.quantize_mx(out=b_q[b][:, cols].bitcast(FP8X4), scales=b_sc[b][:, cols], in_=woven[:])
+
+        def quant_page(b, half, tag):
+            b_q[b, half] = keep.tile([P, BANK], U32, name="b_q", tag=tag, align_bytes=64)
+            b_sc[b, half] = keep.tile([P, BANK], U8, name="b_sc%d%d" % (b, half), align_bytes=64)
+            nc.vector.quantize_mx(out=b_q[b, half][:].bitcast(FP8X4), scales=b_sc[b, half][:], in_=woven[b, half][:])
 
         tiles = H // P
-        rounds = ((), (), (0,), (1,), (2, 3), (4,), (5,), (6,))
-        first_product(0)
-        first_product(1)
+        AHEAD = 3
+        cast_w1(1, 0, 0, nc.scalar.copy)
+        cast_w1(1, 0, 1, nc.scalar.copy)
+        weights_of(0)
+        weights_of(1)
+        for r in range(AHEAD):
+            first_product(r)
+        quant_w1(1, 0, [(0, KP)])
         for r in range(tiles):
-            weights_of(r)
             look_and_fill(r)
-            if r in (1, 2):
-                cast_w1(1, r - 1, 0, nc.scalar.copy)
-                cast_w1(1, r - 1, 1, nc.scalar.copy)
-                quant_w1(1, r - 1, 1)
-            for done in rounds[r]:
-                round_page(done)
-            if r >= 4:
-                cast_w3(*divmod(r - 4, 2))
+            if r == 1:
+                cast_w1(1, 1, 0, nc.scalar.copy)
+                cast_w1(1, 1, 1, nc.scalar.copy)
+                quant_w1(1, 1, [(0, KP)])
+            if 3 <= r < 7:
+                cast_w3(*divmod(r - 3, 2))
+            if r > 1:
+                round_page(r - 2)
             put(r)
             if r + 2 < tiles:
-                first_product(r + 2)
-            if r in (5, 7):
-                quant_w3(r // 6)
-            if r == 6:
-                quant_page(0, 0)
+                weights_of(r + 2)
+            if r + AHEAD < tiles:
+                first_product(r + AHEAD)
+            if r in (5, 6):
+                quant_w3(r - 5)
+        round_page(tiles - 2)
+        weave_page(0, 0, nc.scalar.copy, "woven00")
         round_page(tiles - 1)
-        quant_page(0, 1)
+        quant_page(0, 0, "weight1")
 
         acc_y, acc_d, inner, bent = {}, {}, {}, {}
 
-        def second_pass(c, b):
+        def pass_d(c, b):
             half, nt = divmod(c, N // P)
-            cols = slice(half * BANK, (half + 1) * BANK)
             if b == 0:
                 acc_d[c] = psum.tile([P, BANK], F32, name="acc")
-                acc_y[c] = psum.tile([P, BANK], F32, name="acc")
             nc.tensor.matmul_mx(
                 out=acc_d[c][:],
                 lhsT=w3_q[b][:, nt * P : (nt + 1) * P].bitcast(FP8X4),
                 lhsT_scale=w3_sc[b][:, nt * P : (nt + 1) * P],
-                rhs=b_q[b][:, cols].bitcast(FP8X4), rhs_scale=b_sc[b][:, cols],
+                rhs=b_q[b, half][:].bitcast(FP8X4), rhs_scale=b_sc[b, half][:],
                 start=(b == 0), stop=(b == 1),
             )
+
+        def pass_y(c, b):
+            half, nt = divmod(c, N // P)
+            if b == 0:
+                acc_y[c] = psum.tile([P, BANK], F32, name="acc")
             nc.tensor.matmul_mx(
                 out=acc_y[c][:],
                 lhsT=w2_w[:, b, 2 * nt * P : 2 * (nt + 1) * P].bitcast(FP4X4),
                 lhsT_scale=w2_sc[:, b, nt * P : (nt + 1) * P],
-                rhs=b_q[b][:, cols].bitcast(FP8X4), rhs_scale=b_sc[b][:, cols],
+                rhs=b_q[b, half][:].bitcast(FP8X4), rhs_scale=b_sc[b, half][:],
                 start=(b == 0), stop=(b == 1),
             )
 
         def shift_and_bend(c):
             half, nt = divmod(c, N // P)
-            inner[c] = ring.tile([P, BANK], F32, name="inner")
+            inner[c] = ring.tile([P, BANK], F32, name="inner", bufs=3)
             nc.vector.tensor_tensor(inner[c][:], acc_d[c][:], shift_t[nt][:, half * BANK : (half + 1) * BANK], ALU.add)
             bent[c] = ring.tile([P, BANK], F32, name="bent", bufs=3)
             nc.scalar.activation(out=bent[c][:], in_=inner[c][:], func=ACT.Tanh)
@@ -306,19 +318,32 @@ def tile_list_tipburn_tray_readout_kernel(
         def finish(c):
             half, nt = divmod(c, N // P)
             res = ring.tile([P, BANK], F32, name="res", bufs=4)
-            nc.vector.tensor_tensor(res[:], acc_y[c][:], bent[c][:], ALU.add)
+            if c % 2 == 0:
+                plain = ring.tile([P, BANK], F32, name="plain")
+                nc.scalar.copy(out=plain[:], in_=acc_y[c][:])
+                nc.gpsimd.tensor_tensor(res[:], plain[:], bent[c][:], ALU.add)
+            else:
+                nc.vector.tensor_tensor(res[:], acc_y[c][:], bent[c][:], ALU.add)
             nc.sync.dma_start(out=out[nt * P : (nt + 1) * P, half * BANK : (half + 1) * BANK], in_=res[:])
 
         chunks = 2 * (N // P)
         for c in range(N // P):
-            second_pass(c, 0)
-        quant_page(1, 0)
-        quant_page(1, 1)
+            pass_d(c, 0)
+        weave_page(1, 0, nc.vector.tensor_copy, "woven1")
+        quant_page(1, 0, "b_q10")
+        weave_page(0, 1, nc.scalar.copy, "woven01")
+        weave_page(1, 1, nc.vector.tensor_copy, "woven1")
         for c in range(chunks):
             if c >= N // P:
-                second_pass(c, 0)
-            second_pass(c, 1)
+                pass_d(c, 0)
+            pass_d(c, 1)
             shift_and_bend(c)
+            if c < 2:
+                quant_page(c, 1, "b_q%d1" % c)
             if c > 0:
+                pass_y(c - 1, 0)
+                pass_y(c - 1, 1)
                 finish(c - 1)
+        pass_y(chunks - 1, 0)
+        pass_y(chunks - 1, 1)
         finish(chunks - 1)

from contextlib import ExitStack

import concourse.mybir as mybir

K, T, S, PICK, H, N = 1024, 2048, 1024, 512, 1024, 512
FLOPS = 2 * K * H * S + 2 * 2 * H * N * S

F32 = mybir.dt.float32
BF16 = mybir.dt.bfloat16
I32 = mybir.dt.int32
U32 = mybir.dt.uint32
U16 = mybir.dt.uint16
U8 = mybir.dt.uint8
FP8X4 = mybir.dt.float8_e4m3fn_x4
FP4X4 = mybir.dt.float4_e2m1fn_x4
ALU = mybir.AluOpType
ACT = mybir.ActivationFunctionType

P = 128
PACK = 4
KP = P * PACK
BANK = 512
QUADS = (0, 2, 1, 3)


def tile_list_tipburn_tray_readout_kernel(
    tc, tab_words, tab_scales, offs, pos1, pos2, w1, low, steep, share, mix, skip, wgs, gain,
    w2_words, w2_scales, w3, shift, out,
):
    nc = tc.nc
    with ExitStack() as ctx:
        keep = ctx.enter_context(tc.tile_pool(name="keep", bufs=1))
        ring = ctx.enter_context(tc.tile_pool(name="ring", bufs=2))
        psum = ctx.enter_context(tc.psum_pool(name="psum", bufs=8))

        tab_sc = keep.tile([P, T], U8, name="tab_sc", align_bytes=64)
        nc.gpsimd.memset(tab_sc[:].bitcast(I32), 0)
        tab_w = [keep.tile([P, T], I32, name="tab_w%d" % a, align_bytes=64) for a in range(2)]
        offs_t = keep.tile([P, S // 16], U16, name="offs_t")
        pos1_t = keep.tile([P, PICK // 16], U16, name="pos1_t")
        pos2_t = keep.tile([P, PICK // 16], U16, name="pos2_t")
        nc.sync.dma_start(offs_t[:], offs)
        nc.sync.dma_start(out=tab_w[0][:], in_=tab_words[0].rearrange("p t i -> p (t i)").bitcast(I32))
        for q in QUADS:
            nc.scalar.dma_start(
                out=tab_sc[32 * q : 32 * q + 8, :].bitcast(I32),
                in_=tab_scales[:, 4 * q : 4 * q + 4, :].bitcast(I32),
            )
        nc.sync.dma_start(out=tab_w[1][:], in_=tab_words[1].rearrange("p t i -> p (t i)").bitcast(I32))

        def load_rows(name, vec):
            t = keep.tile([P, H // P], F32, name=name)
            nc.sync.dma_start(
                out=t[:].rearrange("p (b i) -> p b i", i=PACK),
                in_=vec.rearrange("(b p i) -> p b i", p=P, i=PACK),
            )
            return t


        HALF = KP // 2

        def load_w(w, a, c0, name):
            raw = keep.tile([P, PACK, HALF], F32, name=name, tag="raw", bufs=8)
            nc.sync.dma_start(
                out=raw[:],
                in_=w[KP * a : KP * (a + 1), c0 : c0 + HALF].rearrange("(p j) c -> p j c", j=PACK),
            )
            return raw

        w1_raw = {}
        for a in range(2):
            for c in range(2):
                w1_raw[0, a, c] = load_w(w1, a, c * HALF, "w1_raw0%d%d" % (a, c))
        low_t = load_rows("low_t", low)
        steep_t = load_rows("steep_t", steep)
        share_t = load_rows("share_t", share)
        nc.sync.dma_start(pos1_t[:], pos1)
        skip_t = load_rows("skip_t", skip)
        nc.sync.dma_start(pos2_t[:], pos2)

        wgs_t = [keep.tile([P, 2, PICK], F32, name="wgs_t%d" % u) for u in range(2)]
        mix_t = {}

        def load_wgs(u):
            rows = wgs.rearrange("(q i) m -> q i m", i=PACK)[:, 2 * u : 2 * u + 2, :]
            for q in QUADS:
                nc.sync.dma_start(out=wgs_t[u][32 * q : 32 * q + 32, :, :], in_=rows)

        def load_mix(b, u):
            mix_t[b, u] = keep.tile([P, 2, PICK], F32, name="mix_t%d%d" % (b, u))
            rows = mix[KP * b : KP * (b + 1), :].rearrange("(p i) m -> p i m", i=PACK)
            nc.sync.dma_start(out=mix_t[b, u][:], in_=rows[:, 2 * u : 2 * u + 2, :])

        for c in range(2):
            w1_raw[1, 0, c] = load_w(w1, 0, KP + c * HALF, "w1_raw10%d" % c)
        load_wgs(0)
        load_mix(0, 0)
        gain_t = load_rows("gain_t", gain)
        for c in range(2):
            w1_raw[1, 1, c] = load_w(w1, 1, KP + c * HALF, "w1_raw11%d" % c)
        load_wgs(1)
        load_mix(0, 1)
        for u in range(2):
            load_mix(1, u)

        w3_raw = {}
        for b in range(2):
            for c in range(2):
                w3_raw[b, c] = load_w(w3, b, c * HALF, "w3_raw%d%d" % (b, c))
        w2_w = keep.tile([P, 2, 2 * N], U8, name="w2_w", align_bytes=64)
        w2_sc = keep.tile([P, 2, N], U8, name="w2_sc", align_bytes=64)
        nc.gpsimd.memset(w2_sc[:].rearrange("p a c -> p (a c)").bitcast(I32), 0)
        nc.sync.dma_start(out=w2_w[:].bitcast(I32), in_=w2_words.rearrange("a p c -> p a c").bitcast(I32))
        for q in QUADS:
            nc.sync.dma_start(
                out=w2_sc[32 * q : 32 * q + 4, :, :].bitcast(I32),
                in_=w2_scales[:, 4 * q : 4 * q + 4, :].rearrange("a r c -> r a c").bitcast(I32),
            )
        shift_t = []
        for nt in range(N // P):
            st = keep.tile([P, S], F32, name="shift_t%d" % nt)
            nc.sync.dma_start(out=st[:], in_=shift[P * nt : P * (nt + 1), :])
            shift_t.append(st)

        got_w = [keep.tile([P, S], U32, name="got_w%d" % a, align_bytes=64) for a in range(2)]
        got_sc = keep.tile([P, S], U8, name="got_sc", align_bytes=64)
        nc.vector.tensor_copy(got_w[0][:], tab_w[0][:].bitcast(U32).indirect(offs_t[:]))
        nc.vector.tensor_copy(got_sc[:], tab_sc[:].indirect(offs_t[:]))
        nc.vector.tensor_copy(got_w[1][:], tab_w[1][:].bitcast(U32).indirect(offs_t[:]))

        slope = keep.tile([P, H // P], F32, name="slope")
        minus = keep.tile([P, H // P], F32, name="minus")
        nc.gpsimd.tensor_scalar(out=minus[:], in0=steep_t[:], scalar1=-1.0, scalar2=0.0, op0=ALU.mult, op1=ALU.add)
        nc.gpsimd.tensor_tensor(slope[:], minus[:], share_t[:], ALU.mult)

        w_bf = {}
        w1_q, w1_sc, w3_q, w3_sc = {}, {}, {}, {}

        def bf_tile(key):
            if key not in w_bf:
                w_bf[key] = ring.tile([P, KP * PACK], BF16, name="w_bf", align_bytes=64, bufs=3)
            return w_bf[key]

        def cast_w1(b, a, c, copy):
            dst = bf_tile(("w1", b, a))[:].rearrange("p (t m j) -> p m j t", t=PACK, j=PACK)
            m = HALF // PACK
            copy(
                out=dst[:, c * m : (c + 1) * m],
                in_=w1_raw[b, a, c][:].rearrange("p j (m t) -> p m j t", t=PACK),
            )

        def quant_w1(b, a, parts):
            w1_q[b, a] = keep.tile([P, KP], U32, name="w1_q%d%d" % (b, a), align_bytes=64)
            w1_sc[b, a] = keep.tile([P, KP], U8, name="w1_sc%d%d" % (b, a), align_bytes=64)
            for lo, hi in parts:
                nc.vector.quantize_mx(
                    out=w1_q[b, a][:, lo:hi].bitcast(FP8X4),
                    scales=w1_sc[b, a][:, lo:hi],
                    in_=w_bf["w1", b, a][:, PACK * lo : PACK * hi],
                )

        def cast_w3(b, c):
            dst = bf_tile(("w3", b))[:].rearrange("p (m t j) -> p m j t", t=PACK, j=PACK)
            m = HALF // PACK
            nc.scalar.copy(
                out=dst[:, c * m : (c + 1) * m],
                in_=w3_raw[b, c][:].rearrange("p j (m t) -> p m j t", t=PACK),
            )

        def quant_w3(b):
            w3_q[b] = keep.tile([P, N], U32, name="w3_q%d" % b, align_bytes=64)
            w3_sc[b] = keep.tile([P, N], U8, name="w3_sc%d" % b, align_bytes=64)
            nc.vector.quantize_mx(out=w3_q[b][:].bitcast(FP8X4), scales=w3_sc[b][:], in_=w_bf["w3", b][:])

        cast_w1(0, 0, 0, nc.scalar.copy)
        cast_w1(0, 0, 1, nc.scalar.copy)
        quant_w1(0, 0, [(0, KP)])
        cast_w1(0, 1, 0, nc.scalar.copy)
        cast_w1(0, 1, 1, nc.vector.tensor_copy)
        quant_w1(0, 1, [(0, P), (P, KP)])

        tops = keep.tile([P, 2 * (H // P)], F32, name="tops")
        bias = keep.tile([P, H // P], F32, name="bias")
        h_t, look_t, page_t, weight_t = {}, {}, {}, {}
        pairs = {}
        woven, b_q, b_sc = {}, {}, {}

        def first_product(r):
            b, i = divmod(r, PACK)
            h_t[r] = keep.tile([P, S], F32, name="h", tag="turn%d" % ((r + 1) % 4), align_bytes=64)
            for half in range(2):
                cols = slice(half * BANK, (half + 1) * BANK)
                acc = psum.tile([P, BANK], F32, name="acc")
                for a in range(2):
                    nc.tensor.matmul_mx(
                        out=acc[:],
                        lhsT=w1_q[b, a][:, i * P : (i + 1) * P].bitcast(FP8X4),
                        lhsT_scale=w1_sc[b, a][:, i * P : (i + 1) * P],
                        rhs=got_w[a][:, cols].bitcast(FP8X4),
                        rhs_scale=got_sc[PACK * a : P, cols],
                        start=(a == 0),
                        stop=(a == 1),
                    )
                nc.vector.tensor_scalar(
                    out=h_t[r][:, cols], in0=acc[:], scalar1=low_t[:, r : r + 1], scalar2=None,
                    op0=ALU.max, op1=ALU.max, accum_out=tops[:, 2 * r + half : 2 * r + half + 1],
                )
            nc.vector.tensor_scalar(
                out=bias[:, r : r + 1], in0=tops[:, 2 * r : 2 * r + 1],
                scalar1=tops[:, 2 * r + 1 : 2 * r + 2], scalar2=slope[:, r : r + 1],
                op0=ALU.max, op1=ALU.mult,
            )

        def weights_of(r):
            b, i = divmod(r, PACK)
            weight_t[r] = keep.tile([P, PICK], F32, name="weight", tag="weight%d" % (r % 2), align_bytes=64)
            engine = nc.vector if r == H // P - 1 else nc.gpsimd
            engine.tensor_tensor(weight_t[r][:], mix_t[b, i // 2][:, i % 2, :], wgs_t[i // 2][:, i % 2, :], ALU.mult)

        def look_and_fill(r):
            look_t[r] = keep.tile([P, PICK], F32, name="look", tag="turn%d" % (r % 4), align_bytes=64)
            nc.scalar.activation(
                out=look_t[r][:], in_=h_t[r][:].indirect(pos1_t[:]), func=ACT.Sigmoid,
                bias=bias[:, r : r + 1], scale=steep_t[:, r : r + 1],
            )
            page_t[r] = ring.tile([P, S], F32, name="page", bufs=4)
            nc.scalar.activation(out=page_t[r][:], in_=h_t[r][:], func=ACT.Copy, scale=skip_t[:, r : r + 1])

        def put(r):
            nc.vector.tensor_tensor(page_t[r][:].indirect(pos2_t[:]), look_t[r][:], weight_t[r][:], ALU.mult)

        def round_page(r):
            b, i = divmod(r, PACK)
            for half in range(2):
                if i == 0:
                    pairs[b, half] = ring.tile([P, 2, BANK, 2], BF16, name="pairs", bufs=4)
                nc.scalar.activation(
                    out=pairs[b, half][:, i // 2, :, i % 2], in_=page_t[r][:, half * BANK : (half + 1) * BANK],
                    func=ACT.Copy, scale=gain_t[:, r : r + 1],
                )

        def weave_page(b, half, copy, tag):
            woven[b, half] = keep.tile([P, BANK * PACK], BF16, name="woven", tag=tag, align_bytes=64)
            copy(
                out=woven[b, half][:].bitcast(F32).rearrange("p (c e u) -> p c u e", e=PACK, u=2),
                in_=pairs[b, half][:].rearrange("p u c k -> p (u c k)").bitcast(F32).rearrange("p (u c e) -> p c u e", u=2, e=PACK),
            )

        def quant_page(b, half, tag):
            b_q[b, half] = keep.tile([P, BANK], U32, name="b_q", tag=tag, align_bytes=64)
            b_sc[b, half] = keep.tile([P, BANK], U8, name="b_sc%d%d" % (b, half), align_bytes=64)
            nc.vector.quantize_mx(out=b_q[b, half][:].bitcast(FP8X4), scales=b_sc[b, half][:], in_=woven[b, half][:])

        tiles = H // P
        AHEAD = 3
        cast_w1(1, 0, 0, nc.scalar.copy)
        cast_w1(1, 0, 1, nc.scalar.copy)
        weights_of(0)
        weights_of(1)
        for r in range(AHEAD):
            first_product(r)
        quant_w1(1, 0, [(0, KP)])
        for r in range(tiles):
            look_and_fill(r)
            if r == 1:
                cast_w1(1, 1, 0, nc.scalar.copy)
                cast_w1(1, 1, 1, nc.scalar.copy)
                quant_w1(1, 1, [(0, KP)])
            if 3 <= r < 7:
                cast_w3(*divmod(r - 3, 2))
            if r > 1:
                round_page(r - 2)
            put(r)
            if r + 2 < tiles:
                weights_of(r + 2)
            if r + AHEAD < tiles:
                first_product(r + AHEAD)
            if r in (5, 6):
                quant_w3(r - 5)
        round_page(tiles - 2)
        weave_page(0, 0, nc.scalar.copy, "woven00")
        round_page(tiles - 1)
        quant_page(0, 0, "weight1")

        acc_y, acc_d, inner, bent = {}, {}, {}, {}

        def pass_d(c, b):
            half, nt = divmod(c, N // P)
            if b == 0:
                acc_d[c] = psum.tile([P, BANK], F32, name="acc")
            nc.tensor.matmul_mx(
                out=acc_d[c][:],
                lhsT=w3_q[b][:, nt * P : (nt + 1) * P].bitcast(FP8X4),
                lhsT_scale=w3_sc[b][:, nt * P : (nt + 1) * P],
                rhs=b_q[b, half][:].bitcast(FP8X4), rhs_scale=b_sc[b, half][:],
                start=(b == 0), stop=(b == 1),
            )

        def pass_y(c, b):
            half, nt = divmod(c, N // P)
            if b == 0:
                acc_y[c] = psum.tile([P, BANK], F32, name="acc")
            nc.tensor.matmul_mx(
                out=acc_y[c][:],
                lhsT=w2_w[:, b, 2 * nt * P : 2 * (nt + 1) * P].bitcast(FP4X4),
                lhsT_scale=w2_sc[:, b, nt * P : (nt + 1) * P],
                rhs=b_q[b, half][:].bitcast(FP8X4), rhs_scale=b_sc[b, half][:],
                start=(b == 0), stop=(b == 1),
            )

        def shift_and_bend(c):
            half, nt = divmod(c, N // P)
            inner[c] = ring.tile([P, BANK], F32, name="inner", bufs=3)
            nc.vector.tensor_tensor(inner[c][:], acc_d[c][:], shift_t[nt][:, half * BANK : (half + 1) * BANK], ALU.add)
            bent[c] = ring.tile([P, BANK], F32, name="bent", bufs=3)
            nc.scalar.activation(out=bent[c][:], in_=inner[c][:], func=ACT.Tanh)

        def finish(c):
            half, nt = divmod(c, N // P)
            res = ring.tile([P, BANK], F32, name="res", bufs=4)
            if c % 2 == 0:
                plain = ring.tile([P, BANK], F32, name="plain")
                nc.scalar.copy(out=plain[:], in_=acc_y[c][:])
                nc.gpsimd.tensor_tensor(res[:], plain[:], bent[c][:], ALU.add)
            else:
                nc.vector.tensor_tensor(res[:], acc_y[c][:], bent[c][:], ALU.add)
            nc.sync.dma_start(out=out[nt * P : (nt + 1) * P, half * BANK : (half + 1) * BANK], in_=res[:])

        chunks = 2 * (N // P)
        for c in range(N // P):
            pass_d(c, 0)
        weave_page(1, 0, nc.vector.tensor_copy, "woven1")
        quant_page(1, 0, "b_q10")
        weave_page(0, 1, nc.scalar.copy, "woven01")
        weave_page(1, 1, nc.vector.tensor_copy, "woven1")
        for c in range(chunks):
            if c >= N // P:
                pass_d(c, 0)
            pass_d(c, 1)
            shift_and_bend(c)
            if c < 2:
                quant_page(c, 1, "b_q%d1" % c)
            if c > 0:
                pass_y(c - 1, 0)
                pass_y(c - 1, 1)
                finish(c - 1)
        pass_y(chunks - 1, 0)
        pass_y(chunks - 1, 1)
        finish(chunks - 1)
